import numpy as np
import ml_dtypes


def mxq(x, axis, fmt="e4m3"):
    dtype, down = {"e4m3": (ml_dtypes.float8_e4m3fn, 7), "e5m2": (ml_dtypes.float8_e5m2, 14)}[fmt]
    v = np.moveaxis(np.asarray(x, np.float32).astype(ml_dtypes.bfloat16).astype(np.float64), axis, -1)
    blocks = v.reshape(v.shape[:-1] + (-1, 32))
    amax = np.abs(blocks).max(-1, keepdims=True)
    byte = np.maximum(np.where(amax > 0, np.frexp(amax)[1] - 1 + 127, 0) - down, 1)
    scale = np.exp2(byte - 127.0)
    codes = (blocks / scale).astype(np.float32).astype(dtype).astype(np.float64)
    return np.moveaxis((codes * scale).reshape(v.shape), -1, axis)


WIDE = False


def mx_kscale(k):
    if not WIDE:
        return np.ones(k)
    levels = np.array([10, -10, 5, -5, 0])
    if k % 512:
        return np.exp2(np.random.permutation(np.resize(levels, k // 32))).repeat(32)
    a = np.empty((k // 512, 16))
    for p in range(k // 512):
        a[p, :8] = np.random.permutation(np.resize(levels, 8))
        for g in range(8):
            far = levels[np.abs(levels - a[p, g]) >= 10]
            a[p, g + 8] = far[np.random.randint(len(far))]
    return np.exp2(a.ravel()).repeat(32)


def f64(x):
    return np.asarray(x).astype(np.float64)


E2M1 = np.array([0.0, 0.5, 1.0, 1.5, 2.0, 3.0, 4.0, 6.0, -0.0, -0.5, -1.0, -1.5, -2.0, -3.0, -4.0, -6.0])


def pack_weight(w, fmt):
    k, n = w.shape
    w = f64(np.asarray(w, np.float32).astype(ml_dtypes.bfloat16)).reshape(k // 32, 32, n)
    amax = np.abs(w).max(1)
    if fmt == "e4m3":
        byte = np.frexp(amax)[1] - 1 + 127 - 7
    else:
        mant, ex = np.frexp(amax / 6.0)
        byte = np.where(mant > 0.5, ex, ex - 1) + 127
    byte = np.clip(np.where(amax > 0, byte, 1), 1, 254)
    scaled = (w * np.exp2(127.0 - byte)[:, None, :]).reshape(k, n).astype(np.float32)
    by_word = np.ascontiguousarray(scaled.reshape(k // 512, 128, 4, n).transpose(0, 1, 3, 2))
    if fmt == "e4m3":
        words = by_word.astype(ml_dtypes.float8_e4m3fn).view(np.uint8)
    else:
        c = by_word.astype(ml_dtypes.float4_e2m1fn).view(np.uint8) & 0xF
        words = (c[..., 0::2] | (c[..., 1::2] << 4)).reshape(k // 512, 128, 2 * n)
    return np.ascontiguousarray(words), np.ascontiguousarray(byte.astype(np.uint8).reshape(k // 512, 16, n))


def unpack_weight(words, scales, fmt):
    g, _, n = scales.shape
    words = np.ascontiguousarray(words).reshape(g, 128, n, -1)
    if fmt == "e4m3":
        vals = words.view(ml_dtypes.float8_e4m3fn).astype(np.float64)
    else:
        nib = np.empty((g, 128, n, 4), np.uint8)
        nib[..., 0::2] = words & 0xF
        nib[..., 1::2] = words >> 4
        vals = E2M1[nib]
    vals = vals * np.repeat(np.exp2(scales.astype(np.float64) - 127.0), 8, axis=1)[..., None]
    return vals.transpose(0, 1, 3, 2).reshape(g * 512, n)


def bf(x):
    return np.asarray(x, np.float32).astype(ml_dtypes.bfloat16)


def planes(Y):
    r, m = Y.shape
    b = f64(bf(Y)).reshape(r // 32, 32, m)
    amax = np.abs(b).max(1)
    byte = np.clip(np.where(amax > 0, np.frexp(amax)[1] - 1 + 127 - 7, 1), 1, 254)
    codes = (b * np.exp2(127.0 - byte)[:, None, :]).reshape(r, m).astype(np.float32).astype(ml_dtypes.float8_e4m3fn).view(np.uint8)
    words = codes.reshape(r // 512, 128, 4, m).transpose(0, 1, 3, 2)
    return np.ascontiguousarray(words), np.ascontiguousarray(byte.astype(np.uint8).reshape(r // 512, 16, m))


K, L, T, R, N = 1024, 512, 512, 512, 512


def setup_inputs():
    n = np.random.standard_normal
    fk = mx_kscale(K)
    fl = mx_kscale(L)
    fr = mx_kscale(R)
    xtp = pack_weight(n((K, T)) * np.random.uniform(0.3, 1.7, (1, T)) / fk[:, None], "e4m3")
    wap = pack_weight(n((K, R)) * 1 / np.sqrt(K) * fk[:, None], "e4m3")
    xqp = pack_weight(n((L, T)) * 0.5 / fl[:, None], "e2m1")
    wcp = pack_weight(n((L, R)) * 1 / np.sqrt(L) * fl[:, None], "e2m1")
    wbp = pack_weight(n((R, N)) * 1 / np.sqrt(R) / fr[:, None], "e4m3")
    wyp = pack_weight(n((K, N)) * 1 / np.sqrt(K) * fk[:, None], "e2m1")
    return {
        "xt_words": xtp[0],
        "xt_scales": xtp[1],
        "wa_words": wap[0],
        "wa_scales": wap[1],
        "xq_words": xqp[0],
        "xq_scales": xqp[1],
        "wc_words": wcp[0],
        "wc_scales": wcp[1],
        "fr": (np.random.uniform(0.5, 2.0, (R, 1)) * fr[:, None]).astype(np.float32),
        "wb_words": wbp[0],
        "wb_scales": wbp[1],
        "wy_words": wyp[0],
        "wy_scales": wyp[1],
    }


def reference(xt_words, xt_scales, wa_words, wa_scales, xq_words, xq_scales, wc_words, wc_scales, fr, wb_words, wb_scales, wy_words, wy_scales):
    xtu = unpack_weight(xt_words, xt_scales, "e4m3")
    wau = unpack_weight(wa_words, wa_scales, "e4m3")
    xqu = unpack_weight(xq_words, xq_scales, "e2m1")
    wcu = unpack_weight(wc_words, wc_scales, "e2m1")
    wbu = unpack_weight(wb_words, wb_scales, "e4m3")
    wyu = unpack_weight(wy_words, wy_scales, "e2m1")
    z = xtu.T @ wau + xqu.T @ wcu
    d = z - np.mean(z, axis=1, keepdims=True)
    e = d / np.sqrt(np.mean(np.square(d), axis=1, keepdims=True) + 0.01)
    et = e.T
    hid = et * f64(fr)
    hidq = mxq(hid, 0, "e4m3")
    y = wbu.T @ hidq + wyu.T @ xtu
    words, scales = planes(y)
    return y, words, scales

@@ -1,0 +1,254 @@
+from contextlib import ExitStack
+
+import concourse.mybir as mybir
+from concourse.masks import make_identity
+
+K, L, T, R, N = 1024, 512, 512, 512, 512
+FLOPS = 2 * T * R * (K + L) + 2 * N * T * (R + K)
+
+F32 = mybir.dt.float32
+BF16 = mybir.dt.bfloat16
+I32 = mybir.dt.int32
+U8 = mybir.dt.uint8
+FP8X4 = mybir.dt.float8_e4m3fn_x4
+FP4X4 = mybir.dt.float4_e2m1fn_x4
+ACT = mybir.ActivationFunctionType
+ALU = mybir.AluOpType
+
+P = 128
+PACK = 4
+TILES = T // P
+W = 512
+EPS = 0.01
+
+
+def tile_mix_hidden_rows_levelled_pl_kernel(
+    tc, xt_words, xt_scales, wa_words, wa_scales, xq_words, xq_scales, wc_words, wc_scales,
+    fr, wb_words, wb_scales, wy_words, wy_scales, out_0, out_1, out_2,
+):
+    nc = tc.nc
+    with ExitStack() as ctx:
+        sb = ctx.enter_context(tc.tile_pool(name="sb", bufs=1))
+        ps = ctx.enter_context(tc.psum_pool(name="ps", bufs=1))
+        ctx.enter_context(tc.manual_schedule())
+
+        def tile(name, shape, dtype):
+            return sb.tile(shape, dtype, name=name, align_bytes=64)
+
+        rows1 = tile("rows1", [16, 6 * W], U8)
+        planes1 = tile("planes1", [P, 6 * W], U8)
+        rows2 = tile("rows2", [P, 3 * W], U8)
+        rows2d = tile("rows2d", [P, 3 * W], U8)
+        planes2 = tile("planes2", [P, 3 * W], U8)
+        xt_w = tile("xt_w", [P, 2 * W], I32)
+        wa_w = tile("wa_w", [P, 2 * W], I32)
+        xq_w = tile("xq_w", [P, 2 * W], U8)
+        wc_w = tile("wc_w", [P, 2 * W], U8)
+        wy_w = tile("wy_w", [P, 4 * W], U8)
+        wb_w = tile("wb_w", [P, W], I32)
+        wy_d = [tile("wy_d%d" % g, [P, 2 * W], U8) for g in range(2)]
+        wb_d = tile("wb_d", [P, W], I32)
+        fr_sb = tile("fr_sb", [P, PACK], F32)
+        ident = tile("ident", [P, P], F32)
+        warm = tile("warm", [P, 1], F32)
+        warm2 = tile("warm2", [P, 1], F32)
+        y_scales = tile("y_scales", [P, W], U8)
+
+        def load_rows(queue, dst, first, scales):
+            g = scales.shape[0]
+            queue.dma_start(
+                out=dst[0:16, first * W:(first + g) * W].bitcast(I32).rearrange("q (g c) -> q g c", g=g),
+                in_=scales.bitcast(I32).rearrange("g q c -> q g c"),
+            )
+
+        def place_rows(queue, planes, rows):
+            for q in range(4):
+                queue.dma_start(out=planes[32 * q:32 * q + 4, :].bitcast(I32), in_=rows[4 * q:4 * q + 4, :].bitcast(I32))
+
+        nc.vector.memset(warm[:], 1.0)
+        nc.vector.memset(rows2[:].bitcast(I32), 0)
+        nc.vector.memset(planes1[:].bitcast(I32), 0)
+        nc.vector.memset(planes2[:].bitcast(I32), 0)
+        nc.scalar.activation(out=warm2[:], in_=warm[:], func=ACT.Abs_reciprocal_sqrt)
+
+        load_rows(nc.sync, rows1, 0, xt_scales)
+        load_rows(nc.sync, rows1, 2, wa_scales)
+        load_rows(nc.sync, rows1, 4, xq_scales)
+        load_rows(nc.sync, rows1, 5, wc_scales)
+        nc.sync.dma_start(out=xq_w[:].bitcast(I32), in_=xq_words[0].bitcast(I32))
+        nc.sync.dma_start(out=wc_w[:].bitcast(I32), in_=wc_words[0].bitcast(I32))
+        nc.sync.dma_start(out=xt_w[:].rearrange("p (g c) -> p g c", g=2),
+                          in_=xt_words.rearrange("g p c r -> p g (c r)").bitcast(I32))
+        nc.sync.dma_start(out=wa_w[:].rearrange("p (g c) -> p g c", g=2),
+                          in_=wa_words.rearrange("g p c r -> p g (c r)").bitcast(I32))
+        load_rows(nc.gpsimd, rows2, 0, wy_scales)
+        load_rows(nc.gpsimd, rows2, 2, wb_scales)
+        nc.gpsimd.dma_start(out=fr_sb[:], in_=fr.rearrange("(p j) o -> p (j o)", j=PACK))
+        make_identity(nc, ident[:])
+        place_rows(nc.scalar, planes1, rows1)
+        nc.scalar.dma_start(out=wy_w[:].bitcast(I32).rearrange("p (g c) -> p g c", g=2),
+                            in_=wy_words.bitcast(I32).rearrange("g p c -> p g c"))
+        nc.scalar.dma_start(out=wb_w[:], in_=wb_words[0].rearrange("p c r -> p (c r)").bitcast(I32))
+
+        nc.vector.tensor_copy(
+            out=rows2d[:].rearrange("p (i c k) -> p c i k", i=PACK, k=16),
+            in_=rows2[:].rearrange("p (c k i) -> p c i k", i=PACK, k=16),
+        )
+        place_rows(nc.sync, planes2, rows2d)
+
+        def deal_wy(g):
+            nc.vector.tensor_copy(
+                out=wy_d[g][:].rearrange("p (i c k b) -> p c i k b", i=PACK, k=8, b=2),
+                in_=wy_w[:, 2 * W * g:2 * W * (g + 1)].rearrange("p (c k i b) -> p c i k b", i=PACK, k=8, b=2),
+            )
+
+        def deal_wb():
+            nc.vector.tensor_copy(
+                out=wb_d[:].rearrange("p (i c k) -> p c i k", i=PACK, k=4),
+                in_=wb_w[:].rearrange("p (c k i) -> p c i k", i=PACK, k=4),
+            )
+
+        z_ps, stats, nrm, e_sb, et_ps, hid_w, hid_s, y_ps = {}, {}, {}, {}, {}, {}, {}, {}
+
+        def layer1(tt):
+            z_ps[tt] = ps.tile([P, R], F32, name="z%d" % tt, tag="bank%d" % tt)
+            nc.tensor.matmul_mx(
+                out=z_ps[tt][:], lhsT=xq_w[:, 2 * P * tt:2 * P * (tt + 1)].bitcast(FP4X4),
+                lhsT_scale=planes1[:, 4 * W + P * tt:4 * W + P * (tt + 1)],
+                rhs=wc_w[:].bitcast(FP4X4), rhs_scale=planes1[:, 5 * W:6 * W], start=True, stop=False)
+            for g in range(2):
+                nc.tensor.matmul_mx(
+                    out=z_ps[tt][:], lhsT=xt_w[:, g * W + P * tt:g * W + P * (tt + 1)].bitcast(FP8X4),
+                    lhsT_scale=planes1[:, g * W + P * tt:g * W + P * (tt + 1)],
+                    rhs=wa_w[:, g * W:(g + 1) * W].bitcast(FP8X4), rhs_scale=planes1[:, (2 + g) * W:(3 + g) * W],
+                    start=False, stop=(g == 1))
+
+        def row_stats(tt):
+            raw = tile("raw%d" % tt, [P, 6], F32)
+            nc.vector.bn_stats(out=raw[:], in_=z_ps[tt][:])
+            stats[tt] = tile("stats%d" % tt, [P, 2], F32)
+            nc.vector.bn_aggr(out=stats[tt][:], in_=raw[:])
+
+        def negate(tt):
+            nrm[tt] = [tile("nrm%d_%d" % (tt, i), [P, 1], F32) for i in range(3)]
+            nc.vector.tensor_scalar(out=nrm[tt][0][:], in0=stats[tt][:, 0:1], scalar1=-1.0, scalar2=None, op0=ALU.mult)
+
+        def factors(tt):
+            nc.scalar.activation(out=nrm[tt][1][:], in_=stats[tt][:, 1:2], func=ACT.Abs_reciprocal_sqrt, bias=EPS)
+            nc.scalar.activation(out=nrm[tt][2][:], in_=nrm[tt][0][:], func=ACT.Copy, scale=nrm[tt][1][:])
+
+        def level(tt):
+            e_sb[tt] = tile("e%d" % tt, [P, PACK, P], F32)
+            nc.scalar.activation(out=e_sb[tt][:], in_=z_ps[tt][:].rearrange("t (p j) -> t j p", j=PACK),
+                                 func=ACT.Identity, scale=nrm[tt][1][:], bias=nrm[tt][2][:])
+
+        def turn(tt):
+            et_ps[tt] = ps.tile([P, PACK, P], F32, name="et%d" % tt, tag="bank%d" % tt)
+            for j in range(PACK):
+                nc.tensor.transpose(et_ps[tt][:, j, :], e_sb[tt][:, j, :], ident[:])
+
+        hid_bf = {}
+
+        def gain(tt):
+            hid_bf[tt] = tile("hid_bf%d" % tt, [P, P, PACK], BF16)
+            nc.vector.tensor_tensor(
+                out=hid_bf[tt][:], in0=et_ps[tt][:].rearrange("p j t -> p t j"),
+                in1=fr_sb[:].unsqueeze(1).broadcast_to([P, P, PACK]), op=ALU.mult)
+
+        def quant_hid(tt):
+            hid_w[tt] = tile("hid_w%d" % tt, [P, P], I32)
+            hid_s[tt] = tile("hid_s%d" % tt, [P, P], U8)
+            nc.vector.quantize_mx(out=hid_w[tt][:].bitcast(FP8X4), scales=hid_s[tt][:],
+                                  in_=hid_bf[tt][:].rearrange("p t j -> p (t j)"))
+
+        def skip(tt):
+            y_ps[tt] = ps.tile([P, PACK, P], F32, name="y%d" % tt, tag="ybank%d" % tt)
+            for i in range(PACK):
+                for g in range(2):
+                    nc.tensor.matmul_mx(
+                        out=y_ps[tt][:, i, :], lhsT=wy_d[g][:, 2 * P * i:2 * P * (i + 1)].bitcast(FP4X4),
+                        lhsT_scale=planes2[:, (3 * i + g) * P:(3 * i + g + 1) * P],
+                        rhs=xt_w[:, g * W + P * tt:g * W + P * (tt + 1)].bitcast(FP8X4),
+                        rhs_scale=planes1[:, g * W + P * tt:g * W + P * (tt + 1)],
+                        start=(i == 0 and g == 0), stop=False)
+
+        def layer2(tt):
+            for i in range(PACK):
+                nc.tensor.matmul_mx(
+                    out=y_ps[tt][:, i, :], lhsT=wb_d[:, P * i:P * (i + 1)].bitcast(FP8X4),
+                    lhsT_scale=planes2[:, (3 * i + 2) * P:(3 * i + 3) * P],
+                    rhs=hid_w[tt][:].bitcast(FP8X4), rhs_scale=hid_s[tt][:],
+                    start=False, stop=(i == PACK - 1))
+
+        y_bf = {}
+        out_rows = out_0.rearrange("(p i) t -> p i t", i=PACK)
+        out_words = out_1[0].rearrange("p c r -> p (c r)").bitcast(I32)
+
+        def round_y(tt):
+            y_bf[tt] = tile("y_bf%d" % tt, [P, P, PACK], BF16)
+            nc.scalar.copy(out=y_bf[tt][:], in_=y_ps[tt][:].rearrange("p i t -> p t i"))
+
+        y_sb = {}
+
+        def store_y(tt):
+            y_sb[tt] = tile("y_sb%d" % tt, [P, PACK, P], F32)
+            nc.scalar.copy(out=y_sb[tt][:], in_=y_ps[tt][:])
+            nc.sync.dma_start(out=out_rows[:, :, P * tt:P * (tt + 1)], in_=y_sb[tt][:])
+
+        def round_y_sb(tt):
+            y_bf[tt] = tile("y_bf%d" % tt, [P, P, PACK], BF16)
+            nc.vector.tensor_copy(out=y_bf[tt][:].rearrange("p (c k) i -> p c i k", k=4),
+                                  in_=y_sb[tt][:].rearrange("p i (c k) -> p c i k", k=4))
+
+        def quant_y(tt):
+            y_w = tile("y_w%d" % tt, [P, P], I32)
+            nc.vector.quantize_mx(out=y_w[:].bitcast(FP8X4), scales=y_scales[:, P * tt:P * (tt + 1)],
+                                  in_=y_bf[tt][:].rearrange("p t i -> p (t i)"))
+            nc.sync.dma_start(out=out_words[:, P * tt:P * (tt + 1)], in_=y_w[:])
+
+        for tt in range(TILES):
+            layer1(tt)
+        for tt in range(TILES):
+            row_stats(tt)
+            negate(tt)
+            factors(tt)
+            level(tt)
+            if tt < 2:
+                deal_wy(tt)
+            if tt == 2:
+                deal_wb()
+        turn(0)
+        skip(0)
+        gain(0)
+        turn(1)
+        quant_hid(0)
+        gain(1)
+        skip(1)
+        layer2(0)
+        quant_hid(1)
+        turn(2)
+        gain(2)
+        layer2(1)
+        store_y(0)
+        round_y(0)
+        skip(2)
+        quant_hid(2)
+        turn(3)
+        gain(3)
+        layer2(2)
+        store_y(1)
+        round_y(1)
+        quant_y(0)
+        quant_hid(3)
+        skip(3)
+        layer2(3)
+        store_y(2)
+        quant_y(1)
+        round_y_sb(2)
+        store_y(3)
+        quant_y(2)
+        round_y_sb(3)
+        quant_y(3)
+        for q in range(4):
+            queue = nc.sync if q % 2 == 0 else nc.scalar
+            queue.dma_start(out=out_2[0, 4 * q:4 * q + 4, :].bitcast(I32), in_=y_scales[32 * q:32 * q + 4, :].bitcast(I32))

@@ -35,13 +35,13 @@ def tile_mix_hidden_rows_levelled_pl_kernel(
         def tile(name, shape, dtype):
             return sb.tile(shape, dtype, name=name, align_bytes=64)
 
-        rows1 = tile("rows1", [16, 6 * W], U8)
+        rows1 = tile("rows1", [P, 6 * W], U8)
         planes1 = tile("planes1", [P, 6 * W], U8)
         rows2 = tile("rows2", [P, 3 * W], U8)
         rows2d = tile("rows2d", [P, 3 * W], U8)
         planes2 = tile("planes2", [P, 3 * W], U8)
         xt_w = tile("xt_w", [P, 2 * W], I32)
-        wa_w = tile("wa_w", [P, 2 * W], I32)
+        wa_w = [tile("wa_w%d" % g, [P, W], I32) for g in range(2)]
         xq_w = tile("xq_w", [P, 2 * W], U8)
         wc_w = tile("wc_w", [P, 2 * W], U8)
         wy_w = tile("wy_w", [P, 4 * W], U8)
@@ -49,6 +49,7 @@ def tile_mix_hidden_rows_levelled_pl_kernel(
         wy_d = [tile("wy_d%d" % g, [P, 2 * W], U8) for g in range(2)]
         wb_d = tile("wb_d", [P, W], I32)
         fr_sb = tile("fr_sb", [P, PACK], F32)
+        fr_neg = tile("fr_neg", [P, PACK], F32)
         ident = tile("ident", [P, P], F32)
         warm = tile("warm", [P, 1], F32)
         warm2 = tile("warm2", [P, 1], F32)
@@ -65,42 +66,52 @@ def tile_mix_hidden_rows_levelled_pl_kernel(
             for q in range(4):
                 queue.dma_start(out=planes[32 * q:32 * q + 4, :].bitcast(I32), in_=rows[4 * q:4 * q + 4, :].bitcast(I32))
 
-        nc.vector.memset(warm[:], 1.0)
+        nc.vector.memset(rows1[:, 4 * W:5 * W].bitcast(I32), 0)
         nc.vector.memset(rows2[:].bitcast(I32), 0)
         nc.vector.memset(planes1[:].bitcast(I32), 0)
         nc.vector.memset(planes2[:].bitcast(I32), 0)
-        nc.scalar.activation(out=warm2[:], in_=warm[:], func=ACT.Abs_reciprocal_sqrt)
+        nc.vector.memset(warm[:], 1.0)
 
         load_rows(nc.sync, rows1, 0, xt_scales)
+        load_rows(nc.scalar, rows1, 5, wc_scales)
         load_rows(nc.sync, rows1, 2, wa_scales)
-        load_rows(nc.sync, rows1, 4, xq_scales)
-        load_rows(nc.sync, rows1, 5, wc_scales)
+        load_rows(nc.scalar, rows1, 4, xq_scales)
+        nc.sync.dma_start(out=wy_w[:].bitcast(I32).rearrange("p (g c) -> p g c", g=2),
+                          in_=wy_words.bitcast(I32).rearrange("g p c -> p g c"))
         nc.sync.dma_start(out=xq_w[:].bitcast(I32), in_=xq_words[0].bitcast(I32))
         nc.sync.dma_start(out=wc_w[:].bitcast(I32), in_=wc_words[0].bitcast(I32))
         nc.sync.dma_start(out=xt_w[:].rearrange("p (g c) -> p g c", g=2),
                           in_=xt_words.rearrange("g p c r -> p g (c r)").bitcast(I32))
-        nc.sync.dma_start(out=wa_w[:].rearrange("p (g c) -> p g c", g=2),
-                          in_=wa_words.rearrange("g p c r -> p g (c r)").bitcast(I32))
+        nc.sync.dma_start(out=wa_w[0][:], in_=wa_words[0].rearrange("p c r -> p (c r)").bitcast(I32))
         load_rows(nc.gpsimd, rows2, 0, wy_scales)
         load_rows(nc.gpsimd, rows2, 2, wb_scales)
         nc.gpsimd.dma_start(out=fr_sb[:], in_=fr.rearrange("(p j) o -> p (j o)", j=PACK))
         make_identity(nc, ident[:])
+        nc.gpsimd.tensor_scalar(out=fr_neg[:], in0=fr_sb[:], scalar1=-1.0, scalar2=0.0, op0=ALU.mult, op1=ALU.add)
         place_rows(nc.scalar, planes1, rows1)
-        nc.scalar.dma_start(out=wy_w[:].bitcast(I32).rearrange("p (g c) -> p g c", g=2),
-                            in_=wy_words.bitcast(I32).rearrange("g p c -> p g c"))
+        nc.scalar.dma_start(out=wa_w[1][:], in_=wa_words[1].rearrange("p c r -> p (c r)").bitcast(I32))
         nc.scalar.dma_start(out=wb_w[:], in_=wb_words[0].rearrange("p c r -> p (c r)").bitcast(I32))
+        nc.scalar.activation(out=warm2[:], in_=warm[:], func=ACT.Abs_reciprocal_sqrt)
 
-        nc.vector.tensor_copy(
-            out=rows2d[:].rearrange("p (i c k) -> p c i k", i=PACK, k=16),
-            in_=rows2[:].rearrange("p (c k i) -> p c i k", i=PACK, k=16),
-        )
-        place_rows(nc.sync, planes2, rows2d)
+        warm_ps = ps.tile([P, W], F32, name="warm_ps", tag="ybank3")
+        for rep in range(4):
+            nc.tensor.matmul_mx(
+                out=warm_ps[:], lhsT=wy_w[:, 0:2 * P].bitcast(FP4X4), lhsT_scale=rows1[:, 4 * W:4 * W + P],
+                rhs=wy_w[:, 0:2 * W].bitcast(FP4X4), rhs_scale=rows1[:, 4 * W:5 * W], start=True, stop=True)
 
         def deal_wy(g):
             nc.vector.tensor_copy(
                 out=wy_d[g][:].rearrange("p (i c k b) -> p c i k b", i=PACK, k=8, b=2),
                 in_=wy_w[:, 2 * W * g:2 * W * (g + 1)].rearrange("p (c k i b) -> p c i k b", i=PACK, k=8, b=2),
             )
+
+        deal_wy(0)
+        deal_wy(1)
+        nc.vector.tensor_copy(
+            out=rows2d[:].rearrange("p (i c k) -> p c i k", i=PACK, k=16),
+            in_=rows2[:].rearrange("p (c k i) -> p c i k", i=PACK, k=16),
+        )
+        place_rows(nc.sync, planes2, rows2d)
 
         def deal_wb():
             nc.vector.tensor_copy(
@@ -110,32 +121,38 @@ def tile_mix_hidden_rows_levelled_pl_kernel(
 
         z_ps, stats, nrm, e_sb, et_ps, hid_w, hid_s, y_ps = {}, {}, {}, {}, {}, {}, {}, {}
 
-        def layer1(tt):
+        def layer1_q(tt):
             z_ps[tt] = ps.tile([P, R], F32, name="z%d" % tt, tag="bank%d" % tt)
             nc.tensor.matmul_mx(
                 out=z_ps[tt][:], lhsT=xq_w[:, 2 * P * tt:2 * P * (tt + 1)].bitcast(FP4X4),
                 lhsT_scale=planes1[:, 4 * W + P * tt:4 * W + P * (tt + 1)],
                 rhs=wc_w[:].bitcast(FP4X4), rhs_scale=planes1[:, 5 * W:6 * W], start=True, stop=False)
+
+        def layer1_x(tt):
             for g in range(2):
                 nc.tensor.matmul_mx(
                     out=z_ps[tt][:], lhsT=xt_w[:, g * W + P * tt:g * W + P * (tt + 1)].bitcast(FP8X4),
                     lhsT_scale=planes1[:, g * W + P * tt:g * W + P * (tt + 1)],
-                    rhs=wa_w[:, g * W:(g + 1) * W].bitcast(FP8X4), rhs_scale=planes1[:, (2 + g) * W:(3 + g) * W],
+                    rhs=wa_w[g][:].bitcast(FP8X4), rhs_scale=planes1[:, (2 + g) * W:(3 + g) * W],
                     start=False, stop=(g == 1))
 
-        def row_stats(tt):
-            raw = tile("raw%d" % tt, [P, 6], F32)
-            nc.vector.bn_stats(out=raw[:], in_=z_ps[tt][:])
-            stats[tt] = tile("stats%d" % tt, [P, 2], F32)
-            nc.vector.bn_aggr(out=stats[tt][:], in_=raw[:])
+        raw = {}
 
-        def negate(tt):
+        def row_stats(tt):
+            raw[tt] = tile("raw%d" % tt, [P, 6], F32)
+            nc.vector.bn_stats(out=raw[tt][:], in_=z_ps[tt][:])
+
+        def row_aggr(tt):
+            stats[tt] = tile("stats%d" % tt, [P, 2], F32)
+            nc.vector.bn_aggr(out=stats[tt][:], in_=raw[tt][:])
+
+        def inv_spread(tt):
             nrm[tt] = [tile("nrm%d_%d" % (tt, i), [P, 1], F32) for i in range(3)]
-            nc.vector.tensor_scalar(out=nrm[tt][0][:], in0=stats[tt][:, 0:1], scalar1=-1.0, scalar2=None, op0=ALU.mult)
+            nc.scalar.activation(out=nrm[tt][0][:], in_=stats[tt][:, 1:2], func=ACT.Abs_reciprocal_sqrt, bias=EPS)
 
         def factors(tt):
-            nc.scalar.activation(out=nrm[tt][1][:], in_=stats[tt][:, 1:2], func=ACT.Abs_reciprocal_sqrt, bias=EPS)
-            nc.scalar.activation(out=nrm[tt][2][:], in_=nrm[tt][0][:], func=ACT.Copy, scale=nrm[tt][1][:])
+            nc.scalar.activation(out=nrm[tt][1][:], in_=nrm[tt][0][:], func=ACT.Copy, scale=-1.0)
+            nc.scalar.activation(out=nrm[tt][2][:], in_=stats[tt][:, 0:1], func=ACT.Copy, scale=nrm[tt][0][:])
 
         def level(tt):
             e_sb[tt] = tile("e%d" % tt, [P, PACK, P], F32)
@@ -153,7 +170,7 @@ def tile_mix_hidden_rows_levelled_pl_kernel(
             hid_bf[tt] = tile("hid_bf%d" % tt, [P, P, PACK], BF16)
             nc.vector.tensor_tensor(
                 out=hid_bf[tt][:], in0=et_ps[tt][:].rearrange("p j t -> p t j"),
-                in1=fr_sb[:].unsqueeze(1).broadcast_to([P, P, PACK]), op=ALU.mult)
+                in1=fr_neg[:].unsqueeze(1).broadcast_to([P, P, PACK]), op=ALU.mult)
 
         def quant_hid(tt):
             hid_w[tt] = tile("hid_w%d" % tt, [P, P], I32)
@@ -184,16 +201,13 @@ def tile_mix_hidden_rows_levelled_pl_kernel(
         out_rows = out_0.rearrange("(p i) t -> p i t", i=PACK)
         out_words = out_1[0].rearrange("p c r -> p (c r)").bitcast(I32)
 
-        def round_y(tt):
-            y_bf[tt] = tile("y_bf%d" % tt, [P, P, PACK], BF16)
-            nc.scalar.copy(out=y_bf[tt][:], in_=y_ps[tt][:].rearrange("p i t -> p t i"))
-
         y_sb = {}
 
         def store_y(tt):
             y_sb[tt] = tile("y_sb%d" % tt, [P, PACK, P], F32)
             nc.scalar.copy(out=y_sb[tt][:], in_=y_ps[tt][:])
-            nc.sync.dma_start(out=out_rows[:, :, P * tt:P * (tt + 1)], in_=y_sb[tt][:])
+            queue = nc.scalar if tt == TILES - 1 else nc.sync
+            queue.dma_start(out=out_rows[:, :, P * tt:P * (tt + 1)], in_=y_sb[tt][:])
 
         def round_y_sb(tt):
             y_bf[tt] = tile("y_bf%d" % tt, [P, P, PACK], BF16)
@@ -206,47 +220,51 @@ def tile_mix_hidden_rows_levelled_pl_kernel(
                                   in_=y_bf[tt][:].rearrange("p t i -> p (t i)"))
             nc.sync.dma_start(out=out_words[:, P * tt:P * (tt + 1)], in_=y_w[:])
 
+        layer1_q(0)
         for tt in range(TILES):
-            layer1(tt)
+            if tt + 1 < TILES:
+                layer1_q(tt + 1)
+            layer1_x(tt)
         for tt in range(TILES):
             row_stats(tt)
-            negate(tt)
-            factors(tt)
-            level(tt)
-            if tt < 2:
-                deal_wy(tt)
             if tt == 2:
                 deal_wb()
-        turn(0)
+            row_aggr(tt)
+            inv_spread(tt)
+            if tt > 0:
+                level(tt - 1)
+            factors(tt)
+        level(TILES - 1)
         skip(0)
-        gain(0)
-        turn(1)
-        quant_hid(0)
-        gain(1)
         skip(1)
-        layer2(0)
+        turn(0)
+        gain(0)
+        quant_hid(0)
+        turn(1)
+        gain(1)
         quant_hid(1)
+        skip(2)
         turn(2)
         gain(2)
-        layer2(1)
-        store_y(0)
-        round_y(0)
-        skip(2)
         quant_hid(2)
+        layer2(0)
+        store_y(0)
         turn(3)
         gain(3)
-        layer2(2)
-        store_y(1)
-        round_y(1)
-        quant_y(0)
         quant_hid(3)
+        layer2(1)
+        store_y(1)
         skip(3)
-        layer2(3)
+        layer2(2)
         store_y(2)
-        quant_y(1)
+        layer2(3)
+        round_y_sb(0)
+        round_y_sb(1)
+        quant_y(0)
         round_y_sb(2)
-        store_y(3)
+        quant_y(1)
         quant_y(2)
+        store_y(3)
         round_y_sb(3)
         quant_y(3)
         for q in range(4):

@@ -17,9 +17,18 @@ ALU = mybir.AluOpType
 
 P = 128
 PACK = 4
+COLS = 512
 TILES = T // P
-W = 512
+HALF = T // 2
+PASSES = K // (P * PACK)
+BLOCK_ROWS = 16
+QUADRANT = 32
+LINE = 16
 EPS = 0.01
+XT_PLANE, WA_PLANE, XQ_PLANE, WC_PLANE, PLANES_1 = 0, 2, 4, 5, 6
+WY_PLANE, WB_PLANE, PLANES_2 = 0, 2, 3
+WARM_PASSES = 3
+SCALAR_ROUNDS = 2
 
 
 def tile_mix_hidden_rows_levelled_pl_kernel(
@@ -35,136 +44,147 @@ def tile_mix_hidden_rows_levelled_pl_kernel(
         def tile(name, shape, dtype):
             return sb.tile(shape, dtype, name=name, align_bytes=64)
 
-        rows1 = tile("rows1", [P, 6 * W], U8)
-        planes1 = tile("planes1", [P, 6 * W], U8)
-        rows2 = tile("rows2", [P, 3 * W], U8)
-        rows2d = tile("rows2d", [P, 3 * W], U8)
-        planes2 = tile("planes2", [P, 3 * W], U8)
-        xt_w = tile("xt_w", [P, 2 * W], I32)
-        wa_w = [tile("wa_w%d" % g, [P, W], I32) for g in range(2)]
-        xq_w = tile("xq_w", [P, 2 * W], U8)
-        wc_w = tile("wc_w", [P, 2 * W], U8)
-        wy_w = tile("wy_w", [P, 4 * W], U8)
-        wb_w = tile("wb_w", [P, W], I32)
-        wy_d = [tile("wy_d%d" % g, [P, 2 * W], U8) for g in range(2)]
-        wb_d = tile("wb_d", [P, W], I32)
+        def span(index, width):
+            return slice(index * width, (index + 1) * width)
+
+        rows_1 = tile("rows_1", [P, PLANES_1 * COLS], U8)
+        planes_1 = tile("planes_1", [P, PLANES_1 * COLS], U8)
+        rows_2 = tile("rows_2", [P, PLANES_2 * COLS], U8)
+        rows_2_dealt = tile("rows_2_dealt", [P, PLANES_2 * COLS], U8)
+        planes_2 = tile("planes_2", [P, PLANES_2 * COLS], U8)
+        xt_w = [tile("xt_w%d" % h, [P, PASSES * HALF], I32) for h in range(2)]
+        wa_w = tile("wa_w", [P, PASSES * COLS], I32)
+        xq_w = tile("xq_w", [P, 2 * COLS], U8)
+        wc_w = tile("wc_w", [P, 2 * COLS], U8)
+        wy_w = tile("wy_w", [P, PASSES * 2 * COLS], U8)
+        wb_w = tile("wb_w", [P, COLS], I32)
+        wy_dealt = [tile("wy_dealt%d" % g, [P, 2 * COLS], U8) for g in range(PASSES)]
+        wb_dealt = tile("wb_dealt", [P, COLS], I32)
         fr_sb = tile("fr_sb", [P, PACK], F32)
         fr_neg = tile("fr_neg", [P, PACK], F32)
         ident = tile("ident", [P, P], F32)
-        warm = tile("warm", [P, 1], F32)
-        warm2 = tile("warm2", [P, 1], F32)
-        y_scales = tile("y_scales", [P, W], U8)
+        one = tile("one", [P, 1], F32)
+        table_probe = tile("table_probe", [P, 1], F32)
+        y_plane = tile("y_plane", [P, COLS], U8)
 
-        def load_rows(queue, dst, first, scales):
-            g = scales.shape[0]
+        def load_rows(queue, rows, first_plane, scales):
+            passes = scales.shape[0]
+            columns = slice(first_plane * COLS, (first_plane + passes) * COLS)
             queue.dma_start(
-                out=dst[0:16, first * W:(first + g) * W].bitcast(I32).rearrange("q (g c) -> q g c", g=g),
+                out=rows[0:BLOCK_ROWS, columns].bitcast(I32).rearrange("q (g c) -> q g c", g=passes),
                 in_=scales.bitcast(I32).rearrange("g q c -> q g c"),
             )
 
         def place_rows(queue, planes, rows):
-            for q in range(4):
-                queue.dma_start(out=planes[32 * q:32 * q + 4, :].bitcast(I32), in_=rows[4 * q:4 * q + 4, :].bitcast(I32))
+            for q in range(P // QUADRANT):
+                queue.dma_start(out=planes[QUADRANT * q:QUADRANT * q + PACK, :].bitcast(I32),
+                                in_=rows[span(q, PACK), :].bitcast(I32))
 
-        nc.vector.memset(rows1[:, 4 * W:5 * W].bitcast(I32), 0)
-        nc.vector.memset(rows2[:].bitcast(I32), 0)
-        nc.vector.memset(planes1[:].bitcast(I32), 0)
-        nc.vector.memset(planes2[:].bitcast(I32), 0)
-        nc.vector.memset(warm[:], 1.0)
+        def load_passes(queue, dst, words):
+            queue.dma_start(out=dst.rearrange("p (g c) -> p g c", g=words.shape[0]),
+                            in_=words.rearrange("g p c -> p g c"))
 
-        load_rows(nc.sync, rows1, 0, xt_scales)
-        load_rows(nc.scalar, rows1, 5, wc_scales)
-        load_rows(nc.sync, rows1, 2, wa_scales)
-        load_rows(nc.scalar, rows1, 4, xq_scales)
-        nc.sync.dma_start(out=wy_w[:].bitcast(I32).rearrange("p (g c) -> p g c", g=2),
-                          in_=wy_words.bitcast(I32).rearrange("g p c -> p g c"))
-        nc.sync.dma_start(out=xq_w[:].bitcast(I32), in_=xq_words[0].bitcast(I32))
-        nc.sync.dma_start(out=wc_w[:].bitcast(I32), in_=wc_words[0].bitcast(I32))
-        nc.sync.dma_start(out=xt_w[:].rearrange("p (g c) -> p g c", g=2),
-                          in_=xt_words.rearrange("g p c r -> p g (c r)").bitcast(I32))
-        nc.sync.dma_start(out=wa_w[0][:], in_=wa_words[0].rearrange("p c r -> p (c r)").bitcast(I32))
-        load_rows(nc.gpsimd, rows2, 0, wy_scales)
-        load_rows(nc.gpsimd, rows2, 2, wb_scales)
+        def as_words(e4m3_bytes):
+            return e4m3_bytes.rearrange("g p c r -> g p (c r)").bitcast(I32)
+
+        nc.gpsimd.memset(rows_1[:, span(XQ_PLANE, COLS)].bitcast(I32), 0)
+        nc.gpsimd.memset(rows_2[:].bitcast(I32), 0)
+        nc.vector.memset(planes_1[:].bitcast(I32), 0)
+        nc.vector.memset(planes_2[:].bitcast(I32), 0)
+        nc.vector.memset(one[:], 1.0)
+
+        load_rows(nc.sync, rows_1, XT_PLANE, xt_scales)
+        load_rows(nc.scalar, rows_1, WC_PLANE, wc_scales)
+        load_rows(nc.sync, rows_1, WA_PLANE, wa_scales)
+        load_rows(nc.scalar, rows_1, XQ_PLANE, xq_scales)
+        load_passes(nc.sync, wy_w[:].bitcast(I32), wy_words.bitcast(I32))
+        load_passes(nc.sync, xq_w[:].bitcast(I32), xq_words.bitcast(I32))
+        load_passes(nc.sync, wc_w[:].bitcast(I32), wc_words.bitcast(I32))
+        load_passes(nc.sync, wa_w[:], as_words(wa_words))
+        load_rows(nc.gpsimd, rows_2, WY_PLANE, wy_scales)
+        load_rows(nc.gpsimd, rows_2, WB_PLANE, wb_scales)
         nc.gpsimd.dma_start(out=fr_sb[:], in_=fr.rearrange("(p j) o -> p (j o)", j=PACK))
         make_identity(nc, ident[:])
         nc.gpsimd.tensor_scalar(out=fr_neg[:], in0=fr_sb[:], scalar1=-1.0, scalar2=0.0, op0=ALU.mult, op1=ALU.add)
-        place_rows(nc.scalar, planes1, rows1)
-        nc.scalar.dma_start(out=wa_w[1][:], in_=wa_words[1].rearrange("p c r -> p (c r)").bitcast(I32))
-        nc.scalar.dma_start(out=wb_w[:], in_=wb_words[0].rearrange("p c r -> p (c r)").bitcast(I32))
-        nc.scalar.activation(out=warm2[:], in_=warm[:], func=ACT.Abs_reciprocal_sqrt)
+        place_rows(nc.scalar, planes_1, rows_1)
+        for h in range(2):
+            load_passes(nc.scalar, xt_w[h][:], as_words(xt_words)[:, :, span(h, HALF)])
+        load_passes(nc.scalar, wb_w[:], as_words(wb_words))
+        nc.scalar.activation(out=table_probe[:], in_=one[:], func=ACT.Abs_reciprocal_sqrt)
 
-        warm_ps = ps.tile([P, W], F32, name="warm_ps", tag="ybank3")
-        for rep in range(4):
+        warm_ps = ps.tile([P, COLS], F32, name="warm_ps", tag="y_bank%d" % (TILES - 1))
+        for warm_pass in range(WARM_PASSES):
             nc.tensor.matmul_mx(
-                out=warm_ps[:], lhsT=wy_w[:, 0:2 * P].bitcast(FP4X4), lhsT_scale=rows1[:, 4 * W:4 * W + P],
-                rhs=wy_w[:, 0:2 * W].bitcast(FP4X4), rhs_scale=rows1[:, 4 * W:5 * W], start=True, stop=True)
+                out=warm_ps[:], lhsT=wy_w[:, 0:2 * P].bitcast(FP4X4),
+                lhsT_scale=rows_1[:, XQ_PLANE * COLS:XQ_PLANE * COLS + P],
+                rhs=wy_w[:, 0:2 * COLS].bitcast(FP4X4), rhs_scale=rows_1[:, span(XQ_PLANE, COLS)],
+                start=True, stop=True)
 
-        def deal_wy(g):
+        for g in range(PASSES):
             nc.vector.tensor_copy(
-                out=wy_d[g][:].rearrange("p (i c k b) -> p c i k b", i=PACK, k=8, b=2),
-                in_=wy_w[:, 2 * W * g:2 * W * (g + 1)].rearrange("p (c k i b) -> p c i k b", i=PACK, k=8, b=2),
-            )
-
-        deal_wy(0)
-        deal_wy(1)
+                out=wy_dealt[g][:].rearrange("p (i c k b) -> p c i k b", i=PACK, k=LINE // 2, b=2),
+                in_=wy_w[:, span(g, 2 * COLS)].rearrange("p (c k i b) -> p c i k b", i=PACK, k=LINE // 2, b=2))
         nc.vector.tensor_copy(
-            out=rows2d[:].rearrange("p (i c k) -> p c i k", i=PACK, k=16),
-            in_=rows2[:].rearrange("p (c k i) -> p c i k", i=PACK, k=16),
-        )
-        place_rows(nc.sync, planes2, rows2d)
+            out=rows_2_dealt[:].rearrange("p (i c k) -> p c i k", i=PACK, k=LINE),
+            in_=rows_2[:].rearrange("p (c k i) -> p c i k", i=PACK, k=LINE))
+        place_rows(nc.sync, planes_2, rows_2_dealt)
 
         def deal_wb():
             nc.vector.tensor_copy(
-                out=wb_d[:].rearrange("p (i c k) -> p c i k", i=PACK, k=4),
-                in_=wb_w[:].rearrange("p (c k i) -> p c i k", i=PACK, k=4),
-            )
+                out=wb_dealt[:].rearrange("p (i c k) -> p c i k", i=PACK, k=LINE // 4),
+                in_=wb_w[:].rearrange("p (c k i) -> p c i k", i=PACK, k=LINE // 4))
 
-        z_ps, stats, nrm, e_sb, et_ps, hid_w, hid_s, y_ps = {}, {}, {}, {}, {}, {}, {}, {}
+        def plane_1(plane, tt):
+            return planes_1[:, plane * COLS + tt * P:plane * COLS + (tt + 1) * P]
 
-        def layer1_q(tt):
-            z_ps[tt] = ps.tile([P, R], F32, name="z%d" % tt, tag="bank%d" % tt)
+        def plane_2(plane, i):
+            return planes_2[:, span(PLANES_2 * i + plane, P)]
+
+        def xt_codes(g, tt):
+            h, tile_in_half = divmod(tt, TILES // 2)
+            return xt_w[h][:, g * HALF + tile_in_half * P:g * HALF + (tile_in_half + 1) * P].bitcast(FP8X4)
+
+        z_ps, raw_stats, mean_var, inv_std, level_scale, level_bias = {}, {}, {}, {}, {}, {}
+        e_sb, et_ps, hid_bf, hid_w, hid_plane, y_ps, y_sb, y_bf, y_w = {}, {}, {}, {}, {}, {}, {}, {}, {}
+        out_rows = out_0.rearrange("(p i) t -> p i t", i=PACK)
+        out_words = as_words(out_1)[0]
+
+        def layer_1(tt):
+            z_ps[tt] = ps.tile([P, R], F32, name="z%d" % tt, tag="z_bank%d" % tt)
             nc.tensor.matmul_mx(
-                out=z_ps[tt][:], lhsT=xq_w[:, 2 * P * tt:2 * P * (tt + 1)].bitcast(FP4X4),
-                lhsT_scale=planes1[:, 4 * W + P * tt:4 * W + P * (tt + 1)],
-                rhs=wc_w[:].bitcast(FP4X4), rhs_scale=planes1[:, 5 * W:6 * W], start=True, stop=False)
-
-        def layer1_x(tt):
-            for g in range(2):
+                out=z_ps[tt][:], lhsT=xq_w[:, span(tt, 2 * P)].bitcast(FP4X4), lhsT_scale=plane_1(XQ_PLANE, tt),
+                rhs=wc_w[:].bitcast(FP4X4), rhs_scale=planes_1[:, span(WC_PLANE, COLS)], start=True, stop=False)
+            for g in range(PASSES):
                 nc.tensor.matmul_mx(
-                    out=z_ps[tt][:], lhsT=xt_w[:, g * W + P * tt:g * W + P * (tt + 1)].bitcast(FP8X4),
-                    lhsT_scale=planes1[:, g * W + P * tt:g * W + P * (tt + 1)],
-                    rhs=wa_w[g][:].bitcast(FP8X4), rhs_scale=planes1[:, (2 + g) * W:(3 + g) * W],
-                    start=False, stop=(g == 1))
-
-        raw = {}
+                    out=z_ps[tt][:], lhsT=xt_codes(g, tt), lhsT_scale=plane_1(XT_PLANE + g, tt),
+                    rhs=wa_w[:, span(g, COLS)].bitcast(FP8X4), rhs_scale=planes_1[:, span(WA_PLANE + g, COLS)],
+                    start=False, stop=(g == PASSES - 1))
 
         def row_stats(tt):
-            raw[tt] = tile("raw%d" % tt, [P, 6], F32)
-            nc.vector.bn_stats(out=raw[tt][:], in_=z_ps[tt][:])
+            raw_stats[tt] = tile("raw_stats%d" % tt, [P, 6], F32)
+            nc.vector.bn_stats(out=raw_stats[tt][:], in_=z_ps[tt][:])
 
-        def row_aggr(tt):
-            stats[tt] = tile("stats%d" % tt, [P, 2], F32)
-            nc.vector.bn_aggr(out=stats[tt][:], in_=raw[tt][:])
+        def row_spread(tt):
+            mean_var[tt] = tile("mean_var%d" % tt, [P, 2], F32)
+            nc.vector.bn_aggr(out=mean_var[tt][:], in_=raw_stats[tt][:])
+            inv_std[tt] = tile("inv_std%d" % tt, [P, 1], F32)
+            nc.scalar.activation(out=inv_std[tt][:], in_=mean_var[tt][:, 1:2], func=ACT.Abs_reciprocal_sqrt, bias=EPS)
 
-        def inv_spread(tt):
-            nrm[tt] = [tile("nrm%d_%d" % (tt, i), [P, 1], F32) for i in range(3)]
-            nc.scalar.activation(out=nrm[tt][0][:], in_=stats[tt][:, 1:2], func=ACT.Abs_reciprocal_sqrt, bias=EPS)
-
-        def factors(tt):
-            nc.scalar.activation(out=nrm[tt][1][:], in_=nrm[tt][0][:], func=ACT.Copy, scale=-1.0)
-            nc.scalar.activation(out=nrm[tt][2][:], in_=stats[tt][:, 0:1], func=ACT.Copy, scale=nrm[tt][0][:])
+        def level_factors(tt):
+            level_scale[tt] = tile("level_scale%d" % tt, [P, 1], F32)
+            level_bias[tt] = tile("level_bias%d" % tt, [P, 1], F32)
+            nc.scalar.activation(out=level_scale[tt][:], in_=inv_std[tt][:], func=ACT.Copy, scale=-1.0)
+            nc.scalar.activation(out=level_bias[tt][:], in_=mean_var[tt][:, 0:1], func=ACT.Copy, scale=inv_std[tt][:])
 
         def level(tt):
             e_sb[tt] = tile("e%d" % tt, [P, PACK, P], F32)
             nc.scalar.activation(out=e_sb[tt][:], in_=z_ps[tt][:].rearrange("t (p j) -> t j p", j=PACK),
-                                 func=ACT.Identity, scale=nrm[tt][1][:], bias=nrm[tt][2][:])
+                                 func=ACT.Identity, scale=level_scale[tt][:], bias=level_bias[tt][:])
 
         def turn(tt):
-            et_ps[tt] = ps.tile([P, PACK, P], F32, name="et%d" % tt, tag="bank%d" % tt)
+            et_ps[tt] = ps.tile([P, PACK, P], F32, name="et%d" % tt, tag="z_bank%d" % tt)
             for j in range(PACK):
                 nc.tensor.transpose(et_ps[tt][:, j, :], e_sb[tt][:, j, :], ident[:])
-
-        hid_bf = {}
 
         def gain(tt):
             hid_bf[tt] = tile("hid_bf%d" % tt, [P, P, PACK], BF16)
@@ -172,101 +192,87 @@ def tile_mix_hidden_rows_levelled_pl_kernel(
                 out=hid_bf[tt][:], in0=et_ps[tt][:].rearrange("p j t -> p t j"),
                 in1=fr_neg[:].unsqueeze(1).broadcast_to([P, P, PACK]), op=ALU.mult)
 
-        def quant_hid(tt):
+        def quantise_hid(tt):
             hid_w[tt] = tile("hid_w%d" % tt, [P, P], I32)
-            hid_s[tt] = tile("hid_s%d" % tt, [P, P], U8)
-            nc.vector.quantize_mx(out=hid_w[tt][:].bitcast(FP8X4), scales=hid_s[tt][:],
+            hid_plane[tt] = tile("hid_plane%d" % tt, [P, P], U8)
+            nc.vector.quantize_mx(out=hid_w[tt][:].bitcast(FP8X4), scales=hid_plane[tt][:],
                                   in_=hid_bf[tt][:].rearrange("p t j -> p (t j)"))
 
-        def skip(tt):
-            y_ps[tt] = ps.tile([P, PACK, P], F32, name="y%d" % tt, tag="ybank%d" % tt)
+        def skip_product(tt):
+            y_ps[tt] = ps.tile([P, PACK, P], F32, name="y%d" % tt, tag="y_bank%d" % tt)
             for i in range(PACK):
-                for g in range(2):
+                for g in range(PASSES):
                     nc.tensor.matmul_mx(
-                        out=y_ps[tt][:, i, :], lhsT=wy_d[g][:, 2 * P * i:2 * P * (i + 1)].bitcast(FP4X4),
-                        lhsT_scale=planes2[:, (3 * i + g) * P:(3 * i + g + 1) * P],
-                        rhs=xt_w[:, g * W + P * tt:g * W + P * (tt + 1)].bitcast(FP8X4),
-                        rhs_scale=planes1[:, g * W + P * tt:g * W + P * (tt + 1)],
+                        out=y_ps[tt][:, i, :], lhsT=wy_dealt[g][:, span(i, 2 * P)].bitcast(FP4X4),
+                        lhsT_scale=plane_2(WY_PLANE + g, i), rhs=xt_codes(g, tt), rhs_scale=plane_1(XT_PLANE + g, tt),
                         start=(i == 0 and g == 0), stop=False)
 
-        def layer2(tt):
+        def layer_2(tt):
             for i in range(PACK):
                 nc.tensor.matmul_mx(
-                    out=y_ps[tt][:, i, :], lhsT=wb_d[:, P * i:P * (i + 1)].bitcast(FP8X4),
-                    lhsT_scale=planes2[:, (3 * i + 2) * P:(3 * i + 3) * P],
-                    rhs=hid_w[tt][:].bitcast(FP8X4), rhs_scale=hid_s[tt][:],
-                    start=False, stop=(i == PACK - 1))
-
-        y_bf = {}
-        out_rows = out_0.rearrange("(p i) t -> p i t", i=PACK)
-        out_words = out_1[0].rearrange("p c r -> p (c r)").bitcast(I32)
-
-        y_sb = {}
+                    out=y_ps[tt][:, i, :], lhsT=wb_dealt[:, span(i, P)].bitcast(FP8X4), lhsT_scale=plane_2(WB_PLANE, i),
+                    rhs=hid_w[tt][:].bitcast(FP8X4), rhs_scale=hid_plane[tt][:], start=False, stop=(i == PACK - 1))
 
         def store_y(tt):
             y_sb[tt] = tile("y_sb%d" % tt, [P, PACK, P], F32)
             nc.scalar.copy(out=y_sb[tt][:], in_=y_ps[tt][:])
-            queue = nc.scalar if tt == TILES - 1 else nc.sync
-            queue.dma_start(out=out_rows[:, :, P * tt:P * (tt + 1)], in_=y_sb[tt][:])
+            nc.sync.dma_start(out=out_rows[:, :, span(tt, P)], in_=y_sb[tt][:])
 
-        def round_y_sb(tt):
+        def round_y(tt):
             y_bf[tt] = tile("y_bf%d" % tt, [P, P, PACK], BF16)
-            nc.vector.tensor_copy(out=y_bf[tt][:].rearrange("p (c k) i -> p c i k", k=4),
-                                  in_=y_sb[tt][:].rearrange("p i (c k) -> p c i k", k=4))
+            if tt < SCALAR_ROUNDS:
+                nc.scalar.copy(out=y_bf[tt][:], in_=y_ps[tt][:].rearrange("p i t -> p t i"))
+            else:
+                nc.vector.tensor_copy(out=y_bf[tt][:].rearrange("p (c k) i -> p c i k", k=LINE // 4),
+                                      in_=y_sb[tt][:].rearrange("p i (c k) -> p c i k", k=LINE // 4))
 
-        def quant_y(tt):
-            y_w = tile("y_w%d" % tt, [P, P], I32)
-            nc.vector.quantize_mx(out=y_w[:].bitcast(FP8X4), scales=y_scales[:, P * tt:P * (tt + 1)],
+        def quantise_y(tt):
+            pair, place = divmod(tt, 2)
+            if place == 0:
+                y_w[pair] = tile("y_w%d" % pair, [P, 2 * P], I32)
+            nc.vector.quantize_mx(out=y_w[pair][:, span(place, P)].bitcast(FP8X4), scales=y_plane[:, span(tt, P)],
                                   in_=y_bf[tt][:].rearrange("p t i -> p (t i)"))
-            nc.sync.dma_start(out=out_words[:, P * tt:P * (tt + 1)], in_=y_w[:])
+            if place == 1:
+                nc.sync.dma_start(out=out_words[:, span(pair, 2 * P)], in_=y_w[pair][:])
 
-        layer1_q(0)
         for tt in range(TILES):
-            if tt + 1 < TILES:
-                layer1_q(tt + 1)
-            layer1_x(tt)
+            layer_1(tt)
         for tt in range(TILES):
             row_stats(tt)
-            if tt == 2:
+            if tt == TILES - 1:
                 deal_wb()
-            row_aggr(tt)
-            inv_spread(tt)
+            row_spread(tt)
             if tt > 0:
                 level(tt - 1)
-            factors(tt)
+            level_factors(tt)
         level(TILES - 1)
-        skip(0)
-        skip(1)
-        turn(0)
-        gain(0)
-        quant_hid(0)
-        turn(1)
-        gain(1)
-        quant_hid(1)
-        skip(2)
-        turn(2)
-        gain(2)
-        quant_hid(2)
-        layer2(0)
+
+        skip_product(0)
+        for tt in (0, 1):
+            turn(tt)
+            gain(tt)
+            quantise_hid(tt)
+        skip_product(1)
+        layer_2(0)
         store_y(0)
-        turn(3)
-        gain(3)
-        quant_hid(3)
-        layer2(1)
+        round_y(0)
+        for tt in (2, 3):
+            turn(tt)
+            gain(tt)
+            if tt == TILES - 1:
+                quantise_y(0)
+            quantise_hid(tt)
+        layer_2(1)
         store_y(1)
-        skip(3)
-        layer2(2)
-        store_y(2)
-        layer2(3)
-        round_y_sb(0)
-        round_y_sb(1)
-        quant_y(0)
-        round_y_sb(2)
-        quant_y(1)
-        quant_y(2)
-        store_y(3)
-        round_y_sb(3)
-        quant_y(3)
-        for q in range(4):
-            queue = nc.sync if q % 2 == 0 else nc.scalar
-            queue.dma_start(out=out_2[0, 4 * q:4 * q + 4, :].bitcast(I32), in_=y_scales[32 * q:32 * q + 4, :].bitcast(I32))
+        round_y(1)
+        quantise_y(1)
+        for tt in (2, 3):
+            skip_product(tt)
+            layer_2(tt)
+            store_y(tt)
+            round_y(tt)
+            quantise_y(tt)
+        for q in range(P // QUADRANT):
+            queue = nc.scalar if q % 2 == 0 else nc.sync
+            queue.dma_start(out=out_2[0, span(q, PACK), :].bitcast(I32),
+                            in_=y_plane[QUADRANT * q:QUADRANT * q + PACK, :].bitcast(I32))

@@ -21,13 +21,13 @@ COLS = 512
 TILES = T // P
 HALF = T // 2
 PASSES = K // (P * PACK)
-BLOCK_ROWS = 16
+ROW_FIRST, ROW_STEP = 4, 8
 QUADRANT = 32
 LINE = 16
 EPS = 0.01
 XT_PLANE, WA_PLANE, XQ_PLANE, WC_PLANE, PLANES_1 = 0, 2, 4, 5, 6
 WY_PLANE, WB_PLANE, PLANES_2 = 0, 2, 3
-WARM_PASSES = 3
+WARM_PASSES = 4
 SCALAR_ROUNDS = 2
 
 
@@ -71,14 +71,14 @@ def tile_mix_hidden_rows_levelled_pl_kernel(
             passes = scales.shape[0]
             columns = slice(first_plane * COLS, (first_plane + passes) * COLS)
             queue.dma_start(
-                out=rows[0:BLOCK_ROWS, columns].bitcast(I32).rearrange("q (g c) -> q g c", g=passes),
+                out=rows[ROW_FIRST:P:ROW_STEP, columns].bitcast(I32).rearrange("q (g c) -> q g c", g=passes),
                 in_=scales.bitcast(I32).rearrange("g q c -> q g c"),
             )
 
         def place_rows(queue, planes, rows):
-            for q in range(P // QUADRANT):
-                queue.dma_start(out=planes[QUADRANT * q:QUADRANT * q + PACK, :].bitcast(I32),
-                                in_=rows[span(q, PACK), :].bitcast(I32))
+            for s in range(PACK):
+                queue.dma_start(out=planes[s:P:QUADRANT, :].bitcast(I32),
+                                in_=rows[ROW_FIRST + ROW_STEP * s:P:QUADRANT, :].bitcast(I32))
 
         def load_passes(queue, dst, words):
             queue.dma_start(out=dst.rearrange("p (g c) -> p g c", g=words.shape[0]),
@@ -90,7 +90,6 @@ def tile_mix_hidden_rows_levelled_pl_kernel(
         nc.gpsimd.memset(rows_1[:, span(XQ_PLANE, COLS)].bitcast(I32), 0)
         nc.gpsimd.memset(rows_2[:].bitcast(I32), 0)
         nc.vector.memset(planes_1[:].bitcast(I32), 0)
-        nc.vector.memset(planes_2[:].bitcast(I32), 0)
         nc.vector.memset(one[:], 1.0)
 
         load_rows(nc.sync, rows_1, XT_PLANE, xt_scales)
@@ -124,6 +123,7 @@ def tile_mix_hidden_rows_levelled_pl_kernel(
             nc.vector.tensor_copy(
                 out=wy_dealt[g][:].rearrange("p (i c k b) -> p c i k b", i=PACK, k=LINE // 2, b=2),
                 in_=wy_w[:, span(g, 2 * COLS)].rearrange("p (c k i b) -> p c i k b", i=PACK, k=LINE // 2, b=2))
+        nc.vector.memset(planes_2[:].bitcast(I32), 0)
         nc.vector.tensor_copy(
             out=rows_2_dealt[:].rearrange("p (i c k) -> p c i k", i=PACK, k=LINE),
             in_=rows_2[:].rearrange("p (c k i) -> p c i k", i=PACK, k=LINE))

from contextlib import ExitStack

import concourse.mybir as mybir
from concourse.masks import make_identity

K, L, T, R, N = 1024, 512, 512, 512, 512
FLOPS = 2 * T * R * (K + L) + 2 * N * T * (R + K)

F32 = mybir.dt.float32
BF16 = mybir.dt.bfloat16
I32 = mybir.dt.int32
U8 = mybir.dt.uint8
FP8X4 = mybir.dt.float8_e4m3fn_x4
FP4X4 = mybir.dt.float4_e2m1fn_x4
ACT = mybir.ActivationFunctionType
ALU = mybir.AluOpType

P = 128
PACK = 4
COLS = 512
TILES = T // P
HALF = T // 2
PASSES = K // (P * PACK)
ROW_FIRST, ROW_STEP = 4, 8
QUADRANT = 32
LINE = 16
EPS = 0.01
XT_PLANE, WA_PLANE, XQ_PLANE, WC_PLANE, PLANES_1 = 0, 2, 4, 5, 6
WY_PLANE, WB_PLANE, PLANES_2 = 0, 2, 3
WARM_PASSES = 4
SCALAR_ROUNDS = 2


def tile_mix_hidden_rows_levelled_pl_kernel(
    tc, xt_words, xt_scales, wa_words, wa_scales, xq_words, xq_scales, wc_words, wc_scales,
    fr, wb_words, wb_scales, wy_words, wy_scales, out_0, out_1, out_2,
):
    nc = tc.nc
    with ExitStack() as ctx:
        sb = ctx.enter_context(tc.tile_pool(name="sb", bufs=1))
        ps = ctx.enter_context(tc.psum_pool(name="ps", bufs=1))
        ctx.enter_context(tc.manual_schedule())

        def tile(name, shape, dtype):
            return sb.tile(shape, dtype, name=name, align_bytes=64)

        def span(index, width):
            return slice(index * width, (index + 1) * width)

        rows_1 = tile("rows_1", [P, PLANES_1 * COLS], U8)
        planes_1 = tile("planes_1", [P, PLANES_1 * COLS], U8)
        rows_2 = tile("rows_2", [P, PLANES_2 * COLS], U8)
        rows_2_dealt = tile("rows_2_dealt", [P, PLANES_2 * COLS], U8)
        planes_2 = tile("planes_2", [P, PLANES_2 * COLS], U8)
        xt_w = [tile("xt_w%d" % h, [P, PASSES * HALF], I32) for h in range(2)]
        wa_w = tile("wa_w", [P, PASSES * COLS], I32)
        xq_w = tile("xq_w", [P, 2 * COLS], U8)
        wc_w = tile("wc_w", [P, 2 * COLS], U8)
        wy_w = tile("wy_w", [P, PASSES * 2 * COLS], U8)
        wb_w = tile("wb_w", [P, COLS], I32)
        wy_dealt = [tile("wy_dealt%d" % g, [P, 2 * COLS], U8) for g in range(PASSES)]
        wb_dealt = tile("wb_dealt", [P, COLS], I32)
        fr_sb = tile("fr_sb", [P, PACK], F32)
        fr_neg = tile("fr_neg", [P, PACK], F32)
        ident = tile("ident", [P, P], F32)
        one = tile("one", [P, 1], F32)
        table_probe = tile("table_probe", [P, 1], F32)
        y_plane = tile("y_plane", [P, COLS], U8)

        def load_rows(queue, rows, first_plane, scales):
            passes = scales.shape[0]
            columns = slice(first_plane * COLS, (first_plane + passes) * COLS)
            queue.dma_start(
                out=rows[ROW_FIRST:P:ROW_STEP, columns].bitcast(I32).rearrange("q (g c) -> q g c", g=passes),
                in_=scales.bitcast(I32).rearrange("g q c -> q g c"),
            )

        def place_rows(queue, planes, rows):
            for s in range(PACK):
                queue.dma_start(out=planes[s:P:QUADRANT, :].bitcast(I32),
                                in_=rows[ROW_FIRST + ROW_STEP * s:P:QUADRANT, :].bitcast(I32))

        def load_passes(queue, dst, words):
            queue.dma_start(out=dst.rearrange("p (g c) -> p g c", g=words.shape[0]),
                            in_=words.rearrange("g p c -> p g c"))

        def as_words(e4m3_bytes):
            return e4m3_bytes.rearrange("g p c r -> g p (c r)").bitcast(I32)

        nc.gpsimd.memset(rows_1[:, span(XQ_PLANE, COLS)].bitcast(I32), 0)
        nc.gpsimd.memset(rows_2[:].bitcast(I32), 0)
        nc.vector.memset(planes_1[:].bitcast(I32), 0)
        nc.vector.memset(one[:], 1.0)

        load_rows(nc.sync, rows_1, XT_PLANE, xt_scales)
        load_rows(nc.scalar, rows_1, WC_PLANE, wc_scales)
        load_rows(nc.sync, rows_1, WA_PLANE, wa_scales)
        load_rows(nc.scalar, rows_1, XQ_PLANE, xq_scales)
        load_passes(nc.sync, wy_w[:].bitcast(I32), wy_words.bitcast(I32))
        load_passes(nc.sync, xq_w[:].bitcast(I32), xq_words.bitcast(I32))
        load_passes(nc.sync, wc_w[:].bitcast(I32), wc_words.bitcast(I32))
        load_passes(nc.sync, wa_w[:], as_words(wa_words))
        load_rows(nc.gpsimd, rows_2, WY_PLANE, wy_scales)
        load_rows(nc.gpsimd, rows_2, WB_PLANE, wb_scales)
        nc.gpsimd.dma_start(out=fr_sb[:], in_=fr.rearrange("(p j) o -> p (j o)", j=PACK))
        make_identity(nc, ident[:])
        nc.gpsimd.tensor_scalar(out=fr_neg[:], in0=fr_sb[:], scalar1=-1.0, scalar2=0.0, op0=ALU.mult, op1=ALU.add)
        place_rows(nc.scalar, planes_1, rows_1)
        for h in range(2):
            load_passes(nc.scalar, xt_w[h][:], as_words(xt_words)[:, :, span(h, HALF)])
        load_passes(nc.scalar, wb_w[:], as_words(wb_words))
        nc.scalar.activation(out=table_probe[:], in_=one[:], func=ACT.Abs_reciprocal_sqrt)

        warm_ps = ps.tile([P, COLS], F32, name="warm_ps", tag="y_bank%d" % (TILES - 1))
        for warm_pass in range(WARM_PASSES):
            nc.tensor.matmul_mx(
                out=warm_ps[:], lhsT=wy_w[:, 0:2 * P].bitcast(FP4X4),
                lhsT_scale=rows_1[:, XQ_PLANE * COLS:XQ_PLANE * COLS + P],
                rhs=wy_w[:, 0:2 * COLS].bitcast(FP4X4), rhs_scale=rows_1[:, span(XQ_PLANE, COLS)],
                start=True, stop=True)

        for g in range(PASSES):
            nc.vector.tensor_copy(
                out=wy_dealt[g][:].rearrange("p (i c k b) -> p c i k b", i=PACK, k=LINE // 2, b=2),
                in_=wy_w[:, span(g, 2 * COLS)].rearrange("p (c k i b) -> p c i k b", i=PACK, k=LINE // 2, b=2))
        nc.vector.memset(planes_2[:].bitcast(I32), 0)
        nc.vector.tensor_copy(
            out=rows_2_dealt[:].rearrange("p (i c k) -> p c i k", i=PACK, k=LINE),
            in_=rows_2[:].rearrange("p (c k i) -> p c i k", i=PACK, k=LINE))
        place_rows(nc.sync, planes_2, rows_2_dealt)

        def deal_wb():
            nc.vector.tensor_copy(
                out=wb_dealt[:].rearrange("p (i c k) -> p c i k", i=PACK, k=LINE // 4),
                in_=wb_w[:].rearrange("p (c k i) -> p c i k", i=PACK, k=LINE // 4))

        def plane_1(plane, tt):
            return planes_1[:, plane * COLS + tt * P:plane * COLS + (tt + 1) * P]

        def plane_2(plane, i):
            return planes_2[:, span(PLANES_2 * i + plane, P)]

        def xt_codes(g, tt):
            h, tile_in_half = divmod(tt, TILES // 2)
            return xt_w[h][:, g * HALF + tile_in_half * P:g * HALF + (tile_in_half + 1) * P].bitcast(FP8X4)

        z_ps, raw_stats, mean_var, inv_std, level_scale, level_bias = {}, {}, {}, {}, {}, {}
        e_sb, et_ps, hid_bf, hid_w, hid_plane, y_ps, y_sb, y_bf, y_w = {}, {}, {}, {}, {}, {}, {}, {}, {}
        out_rows = out_0.rearrange("(p i) t -> p i t", i=PACK)
        out_words = as_words(out_1)[0]

        def layer_1(tt):
            z_ps[tt] = ps.tile([P, R], F32, name="z%d" % tt, tag="z_bank%d" % tt)
            nc.tensor.matmul_mx(
                out=z_ps[tt][:], lhsT=xq_w[:, span(tt, 2 * P)].bitcast(FP4X4), lhsT_scale=plane_1(XQ_PLANE, tt),
                rhs=wc_w[:].bitcast(FP4X4), rhs_scale=planes_1[:, span(WC_PLANE, COLS)], start=True, stop=False)
            for g in range(PASSES):
                nc.tensor.matmul_mx(
                    out=z_ps[tt][:], lhsT=xt_codes(g, tt), lhsT_scale=plane_1(XT_PLANE + g, tt),
                    rhs=wa_w[:, span(g, COLS)].bitcast(FP8X4), rhs_scale=planes_1[:, span(WA_PLANE + g, COLS)],
                    start=False, stop=(g == PASSES - 1))

        def row_stats(tt):
            raw_stats[tt] = tile("raw_stats%d" % tt, [P, 6], F32)
            nc.vector.bn_stats(out=raw_stats[tt][:], in_=z_ps[tt][:])

        def row_spread(tt):
            mean_var[tt] = tile("mean_var%d" % tt, [P, 2], F32)
            nc.vector.bn_aggr(out=mean_var[tt][:], in_=raw_stats[tt][:])
            inv_std[tt] = tile("inv_std%d" % tt, [P, 1], F32)
            nc.scalar.activation(out=inv_std[tt][:], in_=mean_var[tt][:, 1:2], func=ACT.Abs_reciprocal_sqrt, bias=EPS)

        def level_factors(tt):
            level_scale[tt] = tile("level_scale%d" % tt, [P, 1], F32)
            level_bias[tt] = tile("level_bias%d" % tt, [P, 1], F32)
            nc.scalar.activation(out=level_scale[tt][:], in_=inv_std[tt][:], func=ACT.Copy, scale=-1.0)
            nc.scalar.activation(out=level_bias[tt][:], in_=mean_var[tt][:, 0:1], func=ACT.Copy, scale=inv_std[tt][:])

        def level(tt):
            e_sb[tt] = tile("e%d" % tt, [P, PACK, P], F32)
            nc.scalar.activation(out=e_sb[tt][:], in_=z_ps[tt][:].rearrange("t (p j) -> t j p", j=PACK),
                                 func=ACT.Identity, scale=level_scale[tt][:], bias=level_bias[tt][:])

        def turn(tt):
            et_ps[tt] = ps.tile([P, PACK, P], F32, name="et%d" % tt, tag="z_bank%d" % tt)
            for j in range(PACK):
                nc.tensor.transpose(et_ps[tt][:, j, :], e_sb[tt][:, j, :], ident[:])

        def gain(tt):
            hid_bf[tt] = tile("hid_bf%d" % tt, [P, P, PACK], BF16)
            nc.vector.tensor_tensor(
                out=hid_bf[tt][:], in0=et_ps[tt][:].rearrange("p j t -> p t j"),
                in1=fr_neg[:].unsqueeze(1).broadcast_to([P, P, PACK]), op=ALU.mult)

        def quantise_hid(tt):
            hid_w[tt] = tile("hid_w%d" % tt, [P, P], I32)
            hid_plane[tt] = tile("hid_plane%d" % tt, [P, P], U8)
            nc.vector.quantize_mx(out=hid_w[tt][:].bitcast(FP8X4), scales=hid_plane[tt][:],
                                  in_=hid_bf[tt][:].rearrange("p t j -> p (t j)"))

        def skip_product(tt):
            y_ps[tt] = ps.tile([P, PACK, P], F32, name="y%d" % tt, tag="y_bank%d" % tt)
            for i in range(PACK):
                for g in range(PASSES):
                    nc.tensor.matmul_mx(
                        out=y_ps[tt][:, i, :], lhsT=wy_dealt[g][:, span(i, 2 * P)].bitcast(FP4X4),
                        lhsT_scale=plane_2(WY_PLANE + g, i), rhs=xt_codes(g, tt), rhs_scale=plane_1(XT_PLANE + g, tt),
                        start=(i == 0 and g == 0), stop=False)

        def layer_2(tt):
            for i in range(PACK):
                nc.tensor.matmul_mx(
                    out=y_ps[tt][:, i, :], lhsT=wb_dealt[:, span(i, P)].bitcast(FP8X4), lhsT_scale=plane_2(WB_PLANE, i),
                    rhs=hid_w[tt][:].bitcast(FP8X4), rhs_scale=hid_plane[tt][:], start=False, stop=(i == PACK - 1))

        def store_y(tt):
            y_sb[tt] = tile("y_sb%d" % tt, [P, PACK, P], F32)
            nc.scalar.copy(out=y_sb[tt][:], in_=y_ps[tt][:])
            nc.sync.dma_start(out=out_rows[:, :, span(tt, P)], in_=y_sb[tt][:])

        def round_y(tt):
            y_bf[tt] = tile("y_bf%d" % tt, [P, P, PACK], BF16)
            if tt < SCALAR_ROUNDS:
                nc.scalar.copy(out=y_bf[tt][:], in_=y_ps[tt][:].rearrange("p i t -> p t i"))
            else:
                nc.vector.tensor_copy(out=y_bf[tt][:].rearrange("p (c k) i -> p c i k", k=LINE // 4),
                                      in_=y_sb[tt][:].rearrange("p i (c k) -> p c i k", k=LINE // 4))

        def quantise_y(tt):
            pair, place = divmod(tt, 2)
            if place == 0:
                y_w[pair] = tile("y_w%d" % pair, [P, 2 * P], I32)
            nc.vector.quantize_mx(out=y_w[pair][:, span(place, P)].bitcast(FP8X4), scales=y_plane[:, span(tt, P)],
                                  in_=y_bf[tt][:].rearrange("p t i -> p (t i)"))
            if place == 1:
                nc.sync.dma_start(out=out_words[:, span(pair, 2 * P)], in_=y_w[pair][:])

        for tt in range(TILES):
            layer_1(tt)
        for tt in range(TILES):
            row_stats(tt)
            if tt == TILES - 1:
                deal_wb()
            row_spread(tt)
            if tt > 0:
                level(tt - 1)
            level_factors(tt)
        level(TILES - 1)

        skip_product(0)
        for tt in (0, 1):
            turn(tt)
            gain(tt)
            quantise_hid(tt)
        skip_product(1)
        layer_2(0)
        store_y(0)
        round_y(0)
        for tt in (2, 3):
            turn(tt)
            gain(tt)
            if tt == TILES - 1:
                quantise_y(0)
            quantise_hid(tt)
        layer_2(1)
        store_y(1)
        round_y(1)
        quantise_y(1)
        for tt in (2, 3):
            skip_product(tt)
            layer_2(tt)
            store_y(tt)
            round_y(tt)
            quantise_y(tt)
        for q in range(P // QUADRANT):
            queue = nc.scalar if q % 2 == 0 else nc.sync
            queue.dma_start(out=out_2[0, span(q, PACK), :].bitcast(I32),
                            in_=y_plane[QUADRANT * q:QUADRANT * q + PACK, :].bitcast(I32))
